import numpy as np
import ml_dtypes


def mxq(x, axis, fmt="e4m3"):
    dtype, down = {"e4m3": (ml_dtypes.float8_e4m3fn, 7), "e5m2": (ml_dtypes.float8_e5m2, 14)}[fmt]
    v = np.moveaxis(np.asarray(x, np.float32).astype(ml_dtypes.bfloat16).astype(np.float64), axis, -1)
    blocks = v.reshape(v.shape[:-1] + (-1, 32))
    amax = np.abs(blocks).max(-1, keepdims=True)
    byte = np.maximum(np.where(amax > 0, np.frexp(amax)[1] - 1 + 127, 0) - down, 1)
    scale = np.exp2(byte - 127.0)
    codes = (blocks / scale).astype(np.float32).astype(dtype).astype(np.float64)
    return np.moveaxis((codes * scale).reshape(v.shape), -1, axis)


WIDE = False


def mx_kscale(k):
    if not WIDE:
        return np.ones(k)
    levels = np.array([30, -30])
    if k % 512:
        return np.exp2(np.random.permutation(np.resize(levels, k // 32))).repeat(32)
    a = np.empty((k // 512, 16))
    for p in range(k // 512):
        a[p, :8] = np.random.permutation(np.resize(levels, 8))
        for g in range(8):
            far = levels[np.abs(levels - a[p, g]) >= 10]
            a[p, g + 8] = far[np.random.randint(len(far))]
    return np.exp2(a.ravel()).repeat(32)


def f64(x):
    return np.asarray(x).astype(np.float64)


def striped(idx):
    return np.tile(idx.reshape(-1, 16).T, (8, 1)).astype(np.uint16)


def unstriped(offs):
    return offs[:16].T.reshape(-1).astype(np.int64)


def sigmoid(v):
    return 1.0 / (1.0 + np.exp(-np.maximum(v, -700.0)))


def d_sigmoid(v):
    s = 1.0 / (1.0 + np.exp(-np.maximum(v, -700.0)))
    return s * (1.0 - s)


K, T, E, C, H, N = 128, 2048, 4, 512, 1024, 512


def by_expert(wq, xq):
    return np.concatenate([wq[e].T @ xq[:, e * C:(e + 1) * C] for e in range(E)], axis=1)


def setup_inputs():
    n = np.random.standard_normal
    s = mx_kscale(N)[:, None]
    u = mx_kscale(H)
    return {
        "dyT": (n((N, T)) * s).astype(np.float32),
        "a1": n((H, E * C)).astype(np.float32),
        "a3": n((H, E * C)).astype(np.float32),
        "w2": (n((E, N, H)) / np.sqrt(N) / s[None] * u[None, None, :]).astype(np.float32),
        "w1": (n((E, H, K)) / np.sqrt(H) / u[None, :, None]).astype(np.float32),
        "w3": (n((E, H, K)) / np.sqrt(H) / u[None, :, None]).astype(np.float32),
        "gate": np.tile(np.random.uniform(0.2, 1.0, E * C), (N, 1)).astype(np.float32),
        "offs": striped(np.random.permutation(T)[:E * C]),
    }


def reference(dyT, a1, a3, w2, w1, w3, gate, offs):
    idx = unstriped(offs)
    gq = mxq(f64(gate) * f64(dyT)[:, idx], 0, "e5m2")
    dh = by_expert(mxq(f64(w2), 1, "e4m3"), gq)
    da1 = dh * f64(a3) * d_sigmoid(f64(a1))
    da3 = dh * sigmoid(f64(a1))
    dx = by_expert(mxq(f64(w1), 1, "e4m3"), mxq(da1, 0, "e5m2")) + by_expert(mxq(f64(w3), 1, "e4m3"), mxq(da3, 0, "e5m2"))
    out = np.zeros((K, T))
    out[:, idx] = dx
    return out

@@ -1,0 +1,267 @@
+from contextlib import ExitStack
+
+import concourse.mybir as mybir
+
+K, T, E, C, H, N = 128, 2048, 4, 512, 1024, 512
+FLOPS = 2 * E * C * (N * H + 2 * H * K)
+BYTES = 4 * (N * T + 2 * H * E * C + E * N * H + 2 * E * H * K + E * C + K * T) + 2 * 128 * 128
+
+F32 = mybir.dt.float32
+BF16 = mybir.dt.bfloat16
+U32 = mybir.dt.uint32
+U16 = mybir.dt.uint16
+U8 = mybir.dt.uint8
+E4 = mybir.dt.float8_e4m3fn_x4
+E5 = mybir.dt.float8_e5m2_x4
+ACT = mybir.ActivationFunctionType
+ALU = mybir.AluOpType
+
+P = 128
+R = 4
+KP = P * R
+HP = H // KP
+NP = E * HP
+LEAD = 3
+RAW_BUFS = 15
+
+
+def lanes(x):
+    return x.rearrange("p r (c i) -> p c r i", i=4)
+
+
+def words(x):
+    return x.rearrange("p (c i r) -> p c r i", i=4, r=R)
+
+
+def tile_moe_bdx_glu_sigmoid_kernel(tc, dyT, a1, a3, w2, w1, w3, gate, offs, out):
+    nc = tc.nc
+    with ExitStack() as ctx:
+        held = ctx.enter_context(tc.tile_pool(name="held", bufs=1))
+        rawp = ctx.enter_context(tc.tile_pool(name="rawp", bufs=RAW_BUFS))
+        f32p = ctx.enter_context(tc.tile_pool(name="f32p", bufs=3))
+        two = ctx.enter_context(tc.tile_pool(name="two", bufs=2))
+        three = ctx.enter_context(tc.tile_pool(name="three", bufs=3))
+        dhp = ctx.enter_context(tc.psum_pool(name="dhp", bufs=6))
+        accp = ctx.enter_context(tc.psum_pool(name="accp", bufs=2))
+
+        offsets = held.tile([128, 128], U16, name="offsets")
+        nc.sync.dma_start(offsets[:], offs)
+        window = held.tile([P, T], F32, name="window")
+        gates = []
+        warm = held.tile([P, 8], F32, name="warm")
+        nc.gpsimd.memset(warm[:], 0.0)
+        nc.scalar.activation(warm[:], warm[:], ACT.Sigmoid)
+
+        def lists(e):
+            return offsets[:, e * (C // 16) : (e + 1) * (C // 16)]
+
+        def load_gate(e):
+            g = held.tile([P, C], F32, name="gate%d" % e)
+            nc.sync.dma_start(g[:], gate[0:P, e * C : (e + 1) * C])
+            gates.append(g)
+
+        planes = []
+
+        def load_plane(t):
+            d = rawp.tile([P, T], F32, name="dy", tag="raw", align_bytes=64)
+            nc.sync.dma_start(d[:], dyT.rearrange("(p r) n -> p r n", r=R)[:, t, :])
+            planes.append(d)
+
+        w2raw, a1t, a3t, w13raw = {}, {}, {}, {}
+
+        def load_unit(k):
+            e, h = divmod(k, HP)
+            rows = slice(h * KP, (h + 1) * KP)
+            cols = slice(e * C, (e + 1) * C)
+            w2raw[k] = rawp.tile([P, R, KP], F32, name="w2raw", tag="raw", align_bytes=64)
+            nc.sync.dma_start(w2raw[k][:], w2[e, :, rows].rearrange("(p r) n -> p r n", r=R))
+            a1t[k] = rawp.tile([P, R, C], F32, name="a1t", tag="raw", align_bytes=64)
+            nc.sync.dma_start(a1t[k][:], a1[rows, cols].rearrange("(p r) n -> p r n", r=R))
+            a3t[k] = rawp.tile([P, R, C], F32, name="a3t", tag="raw", align_bytes=64)
+            nc.sync.dma_start(a3t[k][:], a3[rows, cols].rearrange("(p r) n -> p r n", r=R))
+            if h == 0:
+                w13raw[e] = rawp.tile([P, 2 * HP, R, K], F32, name="w13raw", tag="raw", align_bytes=64)
+                for u, w in enumerate((w1, w3)):
+                    nc.sync.dma_start(
+                        w13raw[e][:, u * HP : (u + 1) * HP, :, :],
+                        w[e].rearrange("(h p r) k -> p h r k", h=HP, r=R),
+                    )
+
+        gf, gb, gc, gs = {}, {}, {}, {}
+
+        def gather(e, t):
+            if t == 0:
+                gf[e] = f32p.tile([P, R, C], F32, name="gf", tag="f32", align_bytes=64)
+            nc.vector.tensor_tensor(gf[e][:, t, :], planes[t][:].indirect(lists(e)), gates[e][:], ALU.mult)
+
+        def pack_g(e):
+            gb[e] = two.tile([P, R * C], BF16, name="gb", align_bytes=64)
+            nc.scalar.copy(words(gb[e][:]), lanes(gf[e][:]))
+
+        def quant_g(e):
+            gc[e] = held.tile([P, C], U32, name="gc%d" % e, align_bytes=64)
+            gs[e] = held.tile([P, C], U8, name="gs%d" % e, align_bytes=64)
+            nc.vector.quantize_mx(gc[e][:].bitcast(E5), gs[e][:], gb[e][:])
+
+        w2b, w2c, w2s = {}, {}, {}
+
+        def pack_w2(k):
+            w2b[k] = two.tile([P, R * KP], BF16, name="w2b", align_bytes=64)
+            nc.scalar.copy(
+                w2b[k][:].rearrange("p (t m r) -> p m r t", t=R, r=R),
+                w2raw[k][:].rearrange("p r (m t) -> p m r t", t=R),
+            )
+
+        def quant_w2(k):
+            w2c[k] = three.tile([P, KP], U32, name="w2c", align_bytes=64)
+            w2s[k] = three.tile([P, KP], U8, name="w2s", align_bytes=64)
+            nc.vector.quantize_mx(w2c[k][:].bitcast(E4), w2s[k][:], w2b[k][:])
+
+        w13b, w13c, w13s = {}, {}, {}
+
+        def pack_w13(e):
+            w13b[e] = held.tile([P, 2 * HP * K * R], BF16, name="w13b", align_bytes=64)
+            for u in range(2 * HP):
+                nc.scalar.copy(words(w13b[e][:, u * K * R : (u + 1) * K * R]), lanes(w13raw[e][:, u, :, :]))
+
+        def quant_w13(e):
+            w13c[e] = two.tile([P, 2 * HP * K], U32, name="w13c", align_bytes=64)
+            w13s[e] = two.tile([P, 2 * HP * K], U8, name="w13s", align_bytes=64)
+            nc.vector.quantize_mx(w13c[e][:].bitcast(E4), w13s[e][:], w13b[e][:])
+
+        def gate_s(k):
+            nc.scalar.activation(a1t[k][:], a1t[k][:], ACT.Sigmoid)
+
+        def gate_w(k):
+            nc.vector.scalar_tensor_tensor(a3t[k][:], a1t[k][:], 1.0, a3t[k][:], ALU.subtract, ALU.mult)
+
+        dh = {}
+
+        def mm1(k):
+            e = k // HP
+            dh[k] = []
+            for t in range(R):
+                bank = dhp.tile([P, C], F32, name="dh")
+                cols = slice(t * P, (t + 1) * P)
+                nc.tensor.matmul_mx(
+                    bank[:], w2c[k][:, cols].bitcast(E4), w2s[k][:, cols], gc[e][:].bitcast(E5), gs[e][:], start=True, stop=True
+                )
+                dh[k].append(bank)
+
+        en, d1b, d3b = {}, {}, {}
+
+        def leave(k):
+            en[k] = f32p.tile([P, R, C], F32, name="en", tag="f32", align_bytes=64)
+            for t in range(R):
+                nc.vector.scalar_tensor_tensor(en[k][:, t, :], dh[k][t][:], -1.0, a1t[k][:, t, :], ALU.mult, ALU.mult)
+
+        def pack_d3(k):
+            d3b[k] = two.tile([P, R * C], BF16, name="d3b", align_bytes=64)
+            nc.scalar.activation(words(d3b[k][:]), lanes(en[k][:]), ACT.Copy, scale=-1.0)
+
+        def make_d1(k):
+            d1b[k] = two.tile([P, R * C], BF16, name="d1b", align_bytes=64)
+            nc.vector.tensor_tensor(words(d1b[k][:]), lanes(en[k][:]), lanes(a3t[k][:]), ALU.mult)
+
+        dq = {}
+
+        def quant_d(k):
+            for u, b in enumerate((d1b[k], d3b[k])):
+                c = two.tile([P, C], U32, name="dc%d" % u, align_bytes=64)
+                s = two.tile([P, C], U8, name="ds%d" % u, align_bytes=64)
+                nc.vector.quantize_mx(c[:].bitcast(E5), s[:], b[:])
+                dq[k, u] = (c, s)
+
+        acc, res = {}, {}
+
+        def mm2(k):
+            e, h = divmod(k, HP)
+            if h == 0:
+                acc[e] = accp.tile([K, C], F32, name="acc")
+            for u in range(2):
+                c, s = dq[k, u]
+                cols = slice((u * HP + h) * K, (u * HP + h + 1) * K)
+                nc.tensor.matmul_mx(
+                    acc[e][:],
+                    w13c[e][:, cols].bitcast(E4),
+                    w13s[e][:, cols],
+                    c[:].bitcast(E5),
+                    s[:],
+                    start=(h == 0 and u == 0),
+                    stop=(h == HP - 1 and u == 1),
+                )
+
+        def copy_out(e):
+            res[e] = two.tile([K, C], F32, name="res", align_bytes=64)
+            nc.scalar.copy(res[e][:], acc[e][:])
+
+        def scatter(e):
+            nc.vector.tensor_copy(window[:].indirect(lists(e)), res[e][:])
+
+        load_gate(0)
+        load_plane(0)
+        load_gate(1)
+        load_plane(1)
+        load_plane(2)
+        load_plane(3)
+        load_gate(2)
+        load_gate(3)
+        for k in range(LEAD):
+            load_unit(k)
+
+        for t in range(R):
+            gather(0, t)
+            gather(1, t)
+        pack_g(0)
+        pack_g(1)
+        for t in range(R):
+            gather(2, t)
+        pack_w2(0)
+        quant_g(0)
+        gate_s(0)
+        quant_g(1)
+        quant_w2(0)
+        mm1(0)
+        pack_g(2)
+        for t in range(R):
+            gather(3, t)
+        pack_w2(1)
+        gate_w(0)
+        pack_g(3)
+        quant_g(2)
+        gate_s(1)
+        pack_w13(0)
+        quant_g(3)
+
+        for k in range(NP + 1):
+            e, h = divmod(k, HP)
+            if k + LEAD < NP:
+                load_unit(k + LEAD)
+            if k < NP:
+                leave(k)
+            if k == 0:
+                quant_w13(0)
+            if k > 0:
+                quant_d(k - 1)
+                mm2(k - 1)
+            if k < NP:
+                pack_d3(k)
+            if k > 0 and h == 0:
+                copy_out(e - 1)
+            if k + 1 < NP:
+                quant_w2(k + 1)
+                mm1(k + 1)
+            if k + 2 < NP:
+                pack_w2(k + 2)
+                gate_s(k + 2)
+            if h == 0 and e + 1 < E:
+                pack_w13(e + 1)
+            if k + 1 < NP:
+                gate_w(k + 1)
+            if k > 0 and h == 0:
+                scatter(e - 1)
+            if k < NP:
+                make_d1(k)
+            if h == 1 and e + 1 < E:
+                quant_w13(e + 1)
+        nc.sync.dma_start(out, window[:])

@@ -22,7 +22,8 @@ KP = P * R
 HP = H // KP
 NP = E * HP
 LEAD = 3
-RAW_BUFS = 15
+RAW_BUFS = 14
+HALF = C // 2
 
 
 def lanes(x):
@@ -95,7 +96,7 @@ def tile_moe_bdx_glu_sigmoid_kernel(tc, dyT, a1, a3, w2, w1, w3, gate, offs, out
             nc.vector.tensor_tensor(gf[e][:, t, :], planes[t][:].indirect(lists(e)), gates[e][:], ALU.mult)
 
         def pack_g(e):
-            gb[e] = two.tile([P, R * C], BF16, name="gb", align_bytes=64)
+            gb[e] = two.tile([P, R * C], BF16, name="gb", tag="sb", align_bytes=64)
             nc.scalar.copy(words(gb[e][:]), lanes(gf[e][:]))
 
         def quant_g(e):
@@ -129,11 +130,35 @@ def tile_moe_bdx_glu_sigmoid_kernel(tc, dyT, a1, a3, w2, w1, w3, gate, offs, out
             w13s[e] = two.tile([P, 2 * HP * K], U8, name="w13s", align_bytes=64)
             nc.vector.quantize_mx(w13c[e][:].bitcast(E4), w13s[e][:], w13b[e][:])
 
+        ones = {}
+        w_a, w_b = {}, {}
+        halves = (slice(0, HALF), slice(HALF, C))
+
         def gate_s(k):
+            if k % 2 == 1:
+                ones[k] = held.tile([P, R, C], F32, name="ones", align_bytes=64)
+                nc.scalar.activation(ones[k][:], a1t[k][:], ACT.Sigmoid, scale=-1.0)
             nc.scalar.activation(a1t[k][:], a1t[k][:], ACT.Sigmoid)
 
-        def gate_w(k):
-            nc.vector.scalar_tensor_tensor(a3t[k][:], a1t[k][:], 1.0, a3t[k][:], ALU.subtract, ALU.mult)
+        def gate_w_vec(k, u):
+            o = a3t[k][:, :, halves[u]]
+            if u == 0:
+                w_a[k] = o
+            else:
+                wb = held.tile([P, R, HALF], F32, name="wb", align_bytes=64)
+                o = w_b[k] = wb[:]
+            nc.vector.scalar_tensor_tensor(
+                o, a1t[k][:, :, halves[u]], 1.0, a3t[k][:, :, halves[u]], ALU.subtract, ALU.mult
+            )
+
+        def gate_w_pool(k, u):
+            if u == 0:
+                wa = held.tile([P, R, HALF], F32, name="wa", align_bytes=64)
+                o = w_a[k] = wa[:]
+            else:
+                wb = held.tile([P, R, HALF], F32, name="wb", align_bytes=64)
+                o = w_b[k] = wb[:]
+            nc.gpsimd.tensor_tensor(o, ones[k][:, :, halves[u]], a3t[k][:, :, halves[u]], ALU.mult)
 
         dh = {}
 
@@ -153,20 +178,22 @@ def tile_moe_bdx_glu_sigmoid_kernel(tc, dyT, a1, a3, w2, w1, w3, gate, offs, out
         def leave(k):
             en[k] = f32p.tile([P, R, C], F32, name="en", tag="f32", align_bytes=64)
             for t in range(R):
-                nc.vector.scalar_tensor_tensor(en[k][:, t, :], dh[k][t][:], -1.0, a1t[k][:, t, :], ALU.mult, ALU.mult)
+                nc.vector.scalar_tensor_tensor(en[k][:, t, :], dh[k][t][:], (-1.0, 1.0)[k % 2], a1t[k][:, t, :], ALU.mult, ALU.mult)
 
         def pack_d3(k):
-            d3b[k] = two.tile([P, R * C], BF16, name="d3b", align_bytes=64)
-            nc.scalar.activation(words(d3b[k][:]), lanes(en[k][:]), ACT.Copy, scale=-1.0)
+            d3b[k] = two.tile([P, R * C], BF16, name="d3b", tag="sb", align_bytes=64)
+            nc.scalar.activation(words(d3b[k][:]), lanes(en[k][:]), ACT.Copy, scale=(-1.0, 1.0)[k % 2])
 
         def make_d1(k):
             d1b[k] = two.tile([P, R * C], BF16, name="d1b", align_bytes=64)
-            nc.vector.tensor_tensor(words(d1b[k][:]), lanes(en[k][:]), lanes(a3t[k][:]), ALU.mult)
+            for u, w in enumerate((w_a[k], w_b[k])):
+                cols = slice(u * HALF * R, (u + 1) * HALF * R)
+                nc.vector.tensor_tensor(words(d1b[k][:, cols]), lanes(en[k][:, :, halves[u]]), lanes(w), ALU.mult)
 
         dq = {}
 
         def quant_d(k):
-            for u, b in enumerate((d1b[k], d3b[k])):
+            for u, b in ((1, d3b[k]), (0, d1b[k])):
                 c = two.tile([P, C], U32, name="dc%d" % u, align_bytes=64)
                 s = two.tile([P, C], U8, name="ds%d" % u, align_bytes=64)
                 nc.vector.quantize_mx(c[:].bitcast(E5), s[:], b[:])
@@ -178,7 +205,7 @@ def tile_moe_bdx_glu_sigmoid_kernel(tc, dyT, a1, a3, w2, w1, w3, gate, offs, out
             e, h = divmod(k, HP)
             if h == 0:
                 acc[e] = accp.tile([K, C], F32, name="acc")
-            for u in range(2):
+            for u in (1, 0):
                 c, s = dq[k, u]
                 cols = slice((u * HP + h) * K, (u * HP + h + 1) * K)
                 nc.tensor.matmul_mx(
@@ -187,8 +214,8 @@ def tile_moe_bdx_glu_sigmoid_kernel(tc, dyT, a1, a3, w2, w1, w3, gate, offs, out
                     w13s[e][:, cols],
                     c[:].bitcast(E5),
                     s[:],
-                    start=(h == 0 and u == 0),
-                    stop=(h == HP - 1 and u == 1),
+                    start=(h == 0 and u == 1),
+                    stop=(h == HP - 1 and u == 0),
                 )
 
         def copy_out(e):
@@ -226,7 +253,8 @@ def tile_moe_bdx_glu_sigmoid_kernel(tc, dyT, a1, a3, w2, w1, w3, gate, offs, out
         for t in range(R):
             gather(3, t)
         pack_w2(1)
-        gate_w(0)
+        gate_w_vec(0, 0)
+        gate_w_vec(0, 1)
         pack_g(3)
         quant_g(2)
         gate_s(1)
@@ -237,6 +265,10 @@ def tile_moe_bdx_glu_sigmoid_kernel(tc, dyT, a1, a3, w2, w1, w3, gate, offs, out
             e, h = divmod(k, HP)
             if k + LEAD < NP:
                 load_unit(k + LEAD)
+            if k < NP and h == 1:
+                gate_w_pool(k, 1)
+            if k < NP and h == 0:
+                gate_w_pool(k + 1, 0)
             if k < NP:
                 leave(k)
             if k == 0:
@@ -244,6 +276,8 @@ def tile_moe_bdx_glu_sigmoid_kernel(tc, dyT, a1, a3, w2, w1, w3, gate, offs, out
             if k > 0:
                 quant_d(k - 1)
                 mm2(k - 1)
+            if k == NP:
+                scatter(E - 2)
             if k < NP:
                 pack_d3(k)
             if k > 0 and h == 0:
@@ -256,12 +290,14 @@ def tile_moe_bdx_glu_sigmoid_kernel(tc, dyT, a1, a3, w2, w1, w3, gate, offs, out
                 gate_s(k + 2)
             if h == 0 and e + 1 < E:
                 pack_w13(e + 1)
-            if k + 1 < NP:
-                gate_w(k + 1)
-            if k > 0 and h == 0:
+            if k + 1 < NP and h == 1:
+                gate_w_vec(k + 1, 0)
+            if k > 0 and h == 0 and e != E - 1:
                 scatter(e - 1)
             if k < NP:
                 make_d1(k)
+            if k + 1 < NP and h == 1:
+                gate_w_vec(k + 1, 1)
             if h == 1 and e + 1 < E:
                 quant_w13(e + 1)
         nc.sync.dma_start(out, window[:])

@@ -24,6 +24,7 @@ NP = E * HP
 LEAD = 3
 RAW_BUFS = 14
 HALF = C // 2
+POOL = (3, 5, 7)
 
 
 def lanes(x):
@@ -135,7 +136,7 @@ def tile_moe_bdx_glu_sigmoid_kernel(tc, dyT, a1, a3, w2, w1, w3, gate, offs, out
         halves = (slice(0, HALF), slice(HALF, C))
 
         def gate_s(k):
-            if k % 2 == 1:
+            if k in POOL:
                 ones[k] = held.tile([P, R, C], F32, name="ones", align_bytes=64)
                 nc.scalar.activation(ones[k][:], a1t[k][:], ACT.Sigmoid, scale=-1.0)
             nc.scalar.activation(a1t[k][:], a1t[k][:], ACT.Sigmoid)
@@ -178,11 +179,11 @@ def tile_moe_bdx_glu_sigmoid_kernel(tc, dyT, a1, a3, w2, w1, w3, gate, offs, out
         def leave(k):
             en[k] = f32p.tile([P, R, C], F32, name="en", tag="f32", align_bytes=64)
             for t in range(R):
-                nc.vector.scalar_tensor_tensor(en[k][:, t, :], dh[k][t][:], (-1.0, 1.0)[k % 2], a1t[k][:, t, :], ALU.mult, ALU.mult)
+                nc.vector.scalar_tensor_tensor(en[k][:, t, :], dh[k][t][:], 1.0 if k in POOL else -1.0, a1t[k][:, t, :], ALU.mult, ALU.mult)
 
         def pack_d3(k):
             d3b[k] = two.tile([P, R * C], BF16, name="d3b", tag="sb", align_bytes=64)
-            nc.scalar.activation(words(d3b[k][:]), lanes(en[k][:]), ACT.Copy, scale=(-1.0, 1.0)[k % 2])
+            nc.scalar.activation(words(d3b[k][:]), lanes(en[k][:]), ACT.Copy, scale=1.0 if k in POOL else -1.0)
 
         def make_d1(k):
             d1b[k] = two.tile([P, R * C], BF16, name="d1b", align_bytes=64)
@@ -265,9 +266,9 @@ def tile_moe_bdx_glu_sigmoid_kernel(tc, dyT, a1, a3, w2, w1, w3, gate, offs, out
             e, h = divmod(k, HP)
             if k + LEAD < NP:
                 load_unit(k + LEAD)
-            if k < NP and h == 1:
+            if k in POOL:
                 gate_w_pool(k, 1)
-            if k < NP and h == 0:
+            if k + 1 in POOL:
                 gate_w_pool(k + 1, 0)
             if k < NP:
                 leave(k)
@@ -290,13 +291,13 @@ def tile_moe_bdx_glu_sigmoid_kernel(tc, dyT, a1, a3, w2, w1, w3, gate, offs, out
                 gate_s(k + 2)
             if h == 0 and e + 1 < E:
                 pack_w13(e + 1)
-            if k + 1 < NP and h == 1:
+            if k + 1 < NP and k + 1 not in POOL:
                 gate_w_vec(k + 1, 0)
             if k > 0 and h == 0 and e != E - 1:
                 scatter(e - 1)
             if k < NP:
                 make_d1(k)
-            if k + 1 < NP and h == 1:
+            if k + 1 < NP and k + 1 not in POOL:
                 gate_w_vec(k + 1, 1)
             if h == 1 and e + 1 < E:
                 quant_w13(e + 1)

from contextlib import ExitStack

import concourse.mybir as mybir

K, T, E, C, H, N = 128, 2048, 4, 512, 1024, 512
FLOPS = 2 * E * C * (N * H + 2 * H * K)
BYTES = 4 * (N * T + 2 * H * E * C + E * N * H + 2 * E * H * K + E * C + K * T) + 2 * 128 * 128

F32 = mybir.dt.float32
BF16 = mybir.dt.bfloat16
U32 = mybir.dt.uint32
U16 = mybir.dt.uint16
U8 = mybir.dt.uint8
E4 = mybir.dt.float8_e4m3fn_x4
E5 = mybir.dt.float8_e5m2_x4
ACT = mybir.ActivationFunctionType
ALU = mybir.AluOpType

P = 128
R = 4
KP = P * R
HP = H // KP
NP = E * HP
LEAD = 3
RAW_BUFS = 14
HALF = C // 2
POOL = (3, 5, 7)


def lanes(x):
    return x.rearrange("p r (c i) -> p c r i", i=4)


def words(x):
    return x.rearrange("p (c i r) -> p c r i", i=4, r=R)


def tile_moe_bdx_glu_sigmoid_kernel(tc, dyT, a1, a3, w2, w1, w3, gate, offs, out):
    nc = tc.nc
    with ExitStack() as ctx:
        held = ctx.enter_context(tc.tile_pool(name="held", bufs=1))
        rawp = ctx.enter_context(tc.tile_pool(name="rawp", bufs=RAW_BUFS))
        f32p = ctx.enter_context(tc.tile_pool(name="f32p", bufs=3))
        two = ctx.enter_context(tc.tile_pool(name="two", bufs=2))
        three = ctx.enter_context(tc.tile_pool(name="three", bufs=3))
        dhp = ctx.enter_context(tc.psum_pool(name="dhp", bufs=6))
        accp = ctx.enter_context(tc.psum_pool(name="accp", bufs=2))

        offsets = held.tile([128, 128], U16, name="offsets")
        nc.sync.dma_start(offsets[:], offs)
        window = held.tile([P, T], F32, name="window")
        gates = []
        warm = held.tile([P, 8], F32, name="warm")
        nc.gpsimd.memset(warm[:], 0.0)
        nc.scalar.activation(warm[:], warm[:], ACT.Sigmoid)

        def lists(e):
            return offsets[:, e * (C // 16) : (e + 1) * (C // 16)]

        def load_gate(e):
            g = held.tile([P, C], F32, name="gate%d" % e)
            nc.sync.dma_start(g[:], gate[0:P, e * C : (e + 1) * C])
            gates.append(g)

        planes = []

        def load_plane(t):
            d = rawp.tile([P, T], F32, name="dy", tag="raw", align_bytes=64)
            nc.sync.dma_start(d[:], dyT.rearrange("(p r) n -> p r n", r=R)[:, t, :])
            planes.append(d)

        w2raw, a1t, a3t, w13raw = {}, {}, {}, {}

        def load_unit(k):
            e, h = divmod(k, HP)
            rows = slice(h * KP, (h + 1) * KP)
            cols = slice(e * C, (e + 1) * C)
            w2raw[k] = rawp.tile([P, R, KP], F32, name="w2raw", tag="raw", align_bytes=64)
            nc.sync.dma_start(w2raw[k][:], w2[e, :, rows].rearrange("(p r) n -> p r n", r=R))
            a1t[k] = rawp.tile([P, R, C], F32, name="a1t", tag="raw", align_bytes=64)
            nc.sync.dma_start(a1t[k][:], a1[rows, cols].rearrange("(p r) n -> p r n", r=R))
            a3t[k] = rawp.tile([P, R, C], F32, name="a3t", tag="raw", align_bytes=64)
            nc.sync.dma_start(a3t[k][:], a3[rows, cols].rearrange("(p r) n -> p r n", r=R))
            if h == 0:
                w13raw[e] = rawp.tile([P, 2 * HP, R, K], F32, name="w13raw", tag="raw", align_bytes=64)
                for u, w in enumerate((w1, w3)):
                    nc.sync.dma_start(
                        w13raw[e][:, u * HP : (u + 1) * HP, :, :],
                        w[e].rearrange("(h p r) k -> p h r k", h=HP, r=R),
                    )

        gf, gb, gc, gs = {}, {}, {}, {}

        def gather(e, t):
            if t == 0:
                gf[e] = f32p.tile([P, R, C], F32, name="gf", tag="f32", align_bytes=64)
            nc.vector.tensor_tensor(gf[e][:, t, :], planes[t][:].indirect(lists(e)), gates[e][:], ALU.mult)

        def pack_g(e):
            gb[e] = two.tile([P, R * C], BF16, name="gb", tag="sb", align_bytes=64)
            nc.scalar.copy(words(gb[e][:]), lanes(gf[e][:]))

        def quant_g(e):
            gc[e] = held.tile([P, C], U32, name="gc%d" % e, align_bytes=64)
            gs[e] = held.tile([P, C], U8, name="gs%d" % e, align_bytes=64)
            nc.vector.quantize_mx(gc[e][:].bitcast(E5), gs[e][:], gb[e][:])

        w2b, w2c, w2s = {}, {}, {}

        def pack_w2(k):
            w2b[k] = two.tile([P, R * KP], BF16, name="w2b", align_bytes=64)
            nc.scalar.copy(
                w2b[k][:].rearrange("p (t m r) -> p m r t", t=R, r=R),
                w2raw[k][:].rearrange("p r (m t) -> p m r t", t=R),
            )

        def quant_w2(k):
            w2c[k] = three.tile([P, KP], U32, name="w2c", align_bytes=64)
            w2s[k] = three.tile([P, KP], U8, name="w2s", align_bytes=64)
            nc.vector.quantize_mx(w2c[k][:].bitcast(E4), w2s[k][:], w2b[k][:])

        w13b, w13c, w13s = {}, {}, {}

        def pack_w13(e):
            w13b[e] = held.tile([P, 2 * HP * K * R], BF16, name="w13b", align_bytes=64)
            for u in range(2 * HP):
                nc.scalar.copy(words(w13b[e][:, u * K * R : (u + 1) * K * R]), lanes(w13raw[e][:, u, :, :]))

        def quant_w13(e):
            w13c[e] = two.tile([P, 2 * HP * K], U32, name="w13c", align_bytes=64)
            w13s[e] = two.tile([P, 2 * HP * K], U8, name="w13s", align_bytes=64)
            nc.vector.quantize_mx(w13c[e][:].bitcast(E4), w13s[e][:], w13b[e][:])

        ones = {}
        w_a, w_b = {}, {}
        halves = (slice(0, HALF), slice(HALF, C))

        def gate_s(k):
            if k in POOL:
                ones[k] = held.tile([P, R, C], F32, name="ones", align_bytes=64)
                nc.scalar.activation(ones[k][:], a1t[k][:], ACT.Sigmoid, scale=-1.0)
            nc.scalar.activation(a1t[k][:], a1t[k][:], ACT.Sigmoid)

        def gate_w_vec(k, u):
            o = a3t[k][:, :, halves[u]]
            if u == 0:
                w_a[k] = o
            else:
                wb = held.tile([P, R, HALF], F32, name="wb", align_bytes=64)
                o = w_b[k] = wb[:]
            nc.vector.scalar_tensor_tensor(
                o, a1t[k][:, :, halves[u]], 1.0, a3t[k][:, :, halves[u]], ALU.subtract, ALU.mult
            )

        def gate_w_pool(k, u):
            if u == 0:
                wa = held.tile([P, R, HALF], F32, name="wa", align_bytes=64)
                o = w_a[k] = wa[:]
            else:
                wb = held.tile([P, R, HALF], F32, name="wb", align_bytes=64)
                o = w_b[k] = wb[:]
            nc.gpsimd.tensor_tensor(o, ones[k][:, :, halves[u]], a3t[k][:, :, halves[u]], ALU.mult)

        dh = {}

        def mm1(k):
            e = k // HP
            dh[k] = []
            for t in range(R):
                bank = dhp.tile([P, C], F32, name="dh")
                cols = slice(t * P, (t + 1) * P)
                nc.tensor.matmul_mx(
                    bank[:], w2c[k][:, cols].bitcast(E4), w2s[k][:, cols], gc[e][:].bitcast(E5), gs[e][:], start=True, stop=True
                )
                dh[k].append(bank)

        en, d1b, d3b = {}, {}, {}

        def leave(k):
            en[k] = f32p.tile([P, R, C], F32, name="en", tag="f32", align_bytes=64)
            for t in range(R):
                nc.vector.scalar_tensor_tensor(en[k][:, t, :], dh[k][t][:], 1.0 if k in POOL else -1.0, a1t[k][:, t, :], ALU.mult, ALU.mult)

        def pack_d3(k):
            d3b[k] = two.tile([P, R * C], BF16, name="d3b", tag="sb", align_bytes=64)
            nc.scalar.activation(words(d3b[k][:]), lanes(en[k][:]), ACT.Copy, scale=1.0 if k in POOL else -1.0)

        def make_d1(k):
            d1b[k] = two.tile([P, R * C], BF16, name="d1b", align_bytes=64)
            for u, w in enumerate((w_a[k], w_b[k])):
                cols = slice(u * HALF * R, (u + 1) * HALF * R)
                nc.vector.tensor_tensor(words(d1b[k][:, cols]), lanes(en[k][:, :, halves[u]]), lanes(w), ALU.mult)

        dq = {}

        def quant_d(k):
            for u, b in ((1, d3b[k]), (0, d1b[k])):
                c = two.tile([P, C], U32, name="dc%d" % u, align_bytes=64)
                s = two.tile([P, C], U8, name="ds%d" % u, align_bytes=64)
                nc.vector.quantize_mx(c[:].bitcast(E5), s[:], b[:])
                dq[k, u] = (c, s)

        acc, res = {}, {}

        def mm2(k):
            e, h = divmod(k, HP)
            if h == 0:
                acc[e] = accp.tile([K, C], F32, name="acc")
            for u in (1, 0):
                c, s = dq[k, u]
                cols = slice((u * HP + h) * K, (u * HP + h + 1) * K)
                nc.tensor.matmul_mx(
                    acc[e][:],
                    w13c[e][:, cols].bitcast(E4),
                    w13s[e][:, cols],
                    c[:].bitcast(E5),
                    s[:],
                    start=(h == 0 and u == 1),
                    stop=(h == HP - 1 and u == 0),
                )

        def copy_out(e):
            res[e] = two.tile([K, C], F32, name="res", align_bytes=64)
            nc.scalar.copy(res[e][:], acc[e][:])

        def scatter(e):
            nc.vector.tensor_copy(window[:].indirect(lists(e)), res[e][:])

        load_gate(0)
        load_plane(0)
        load_gate(1)
        load_plane(1)
        load_plane(2)
        load_plane(3)
        load_gate(2)
        load_gate(3)
        for k in range(LEAD):
            load_unit(k)

        for t in range(R):
            gather(0, t)
            gather(1, t)
        pack_g(0)
        pack_g(1)
        for t in range(R):
            gather(2, t)
        pack_w2(0)
        quant_g(0)
        gate_s(0)
        quant_g(1)
        quant_w2(0)
        mm1(0)
        pack_g(2)
        for t in range(R):
            gather(3, t)
        pack_w2(1)
        gate_w_vec(0, 0)
        gate_w_vec(0, 1)
        pack_g(3)
        quant_g(2)
        gate_s(1)
        pack_w13(0)
        quant_g(3)

        for k in range(NP + 1):
            e, h = divmod(k, HP)
            if k + LEAD < NP:
                load_unit(k + LEAD)
            if k in POOL:
                gate_w_pool(k, 1)
            if k + 1 in POOL:
                gate_w_pool(k + 1, 0)
            if k < NP:
                leave(k)
            if k == 0:
                quant_w13(0)
            if k > 0:
                quant_d(k - 1)
                mm2(k - 1)
            if k == NP:
                scatter(E - 2)
            if k < NP:
                pack_d3(k)
            if k > 0 and h == 0:
                copy_out(e - 1)
            if k + 1 < NP:
                quant_w2(k + 1)
                mm1(k + 1)
            if k + 2 < NP:
                pack_w2(k + 2)
                gate_s(k + 2)
            if h == 0 and e + 1 < E:
                pack_w13(e + 1)
            if k + 1 < NP and k + 1 not in POOL:
                gate_w_vec(k + 1, 0)
            if k > 0 and h == 0 and e != E - 1:
                scatter(e - 1)
            if k < NP:
                make_d1(k)
            if k + 1 < NP and k + 1 not in POOL:
                gate_w_vec(k + 1, 1)
            if h == 1 and e + 1 < E:
                quant_w13(e + 1)
        nc.sync.dma_start(out, window[:])
